import numpy as np
CORES = [5,13,21,29,37,45,53,61,69,77,85,93,101,109,117,125,133,141,149,157,165,173,181,189,197,205,213,221,229,237,245,253,261,269,277,285,293,301,309,317,325,333,341,349,357,365,373,381,389,397,405,413,421,429,437,445,453,461,469,477,485,493,501,509]
N = 64
WIDTHS = [128 if 32 <= r < 36 else 4 for r in range(N)]
def setup_inputs(rng):
    return {"x": rng.standard_normal((N, 128, 128), dtype=np.float32)}
def reference(x):
    g = np.concatenate([x[r][:, :WIDTHS[r]] for r in range(N)], axis=1)
    return {"y": np.broadcast_to(g, (N,) + g.shape)}

@@ -1,0 +1,192 @@
+from concourse.bass import DstId, RemoteDMATransfer
+
+TOTAL = 752
+SCRATCH = {
+    "land": ("sbuf", [128, TOTAL], "float32"),
+}
+SEMAPHORES = ["loaded", "read", "stored", "sh", "asm", "rl", "hf", "fin"]
+CACHE = {}
+
+
+def world(h, q, j, c):
+    return h * 128 + (2 * j + q) * 8 + c
+
+
+def build_sends(widths):
+    off = [0]
+    for w in widths:
+        off.append(off[-1] + w)
+    sends = []
+
+    def send(src, sem, c0, c1, dsts):
+        if dsts and c1 > c0:
+            sends.append([src, sem, c0, c1, list(dsts)])
+
+    def final(asm_core, h, q, j, c0, c1):
+        full = []
+        for qq in (q, 1 - q):
+            r = 16 * h + 2 * j + qq
+            o0, o1 = off[r], off[r + 1]
+            dst = world(h, qq, j, 5)
+            if o1 <= c0 or o0 >= c1:
+                full.append(dst)
+            else:
+                send(asm_core, "fin", c0, o0, [dst])
+                send(asm_core, "fin", o1, c1, [dst])
+        send(asm_core, "fin", c0, c1, full)
+
+    for x in range(4):
+        p = 0 if x < 2 else 1
+        c = 7 if x in (0, 2) else 3
+        js = [j for j in range(8) if widths[16 * x + 2 * j] == 4]
+        seg0, seg1 = off[16 * x + 2 * js[0]], off[16 * x + 16]
+        for j in js:
+            own = {h: world(h, p, j, c) for h in range(4)}
+            ox, oi, oc, od = own[x], own[x ^ 1], own[3 - x], own[x ^ 2]
+            cs, co = off[16 * x + 2 * j + p], off[16 * x + 2 * j + 1 - p]
+            p0 = min(cs, co)
+            first = [ox, oi] if x < 2 else [ox, oi, oc]
+            relay = world(x, 1 - p, j, 6)
+            send(world(x, p, j, 5), "hf", cs, cs + 4, first)
+            send(world(x, 1 - p, j, 5), "rl", co, co + 4, [relay])
+            send(relay, "hf", co, co + 4, first)
+            if x < 2:
+                send(ox, "hf", p0, p0 + 8, [oc])
+                send(oi, "hf", p0, p0 + 8, [od])
+            else:
+                send(oc, "hf", p0, p0 + 8, [od])
+            for h in range(4):
+                send(own[h], "asm", p0, p0 + 8, [world(h, p, jj, c) for jj in range(8) if jj != j])
+        for h in range(4):
+            for j in range(8):
+                final(world(h, p, j, c), h, p, j, seg0, seg1)
+
+    for i in range(4):
+        q, js = i % 2, i // 2
+        base = off[32 + i]
+        ac = 6 if i < 2 else 2
+        src = world(2, q, js, 5)
+        for j in range(8):
+            a = j % 2 == js % 2
+            s0, s1 = base + 16 * j, base + 16 * j + 16
+            oc = {0: 0 if a else 4, 1: 0 if a else 4, 2: 0 if a else 4, 3: 4 if a else 0}
+            own = {h: world(h, q, j, oc[h]) for h in range(4)}
+            if a:
+                send(src, "sh", s0, s1, [own[2]])
+                send(own[2], "sh", s0, s1, [own[1], own[3]])
+                send(own[1], "sh", s0, s1, [own[0]])
+            else:
+                send(src, "sh", s0, s1, [own[3]])
+                send(own[3], "sh", s0, s1, [own[2], own[0]])
+                send(own[0], "sh", s0, s1, [own[1]])
+            for h in range(4):
+                send(own[h], "asm", s0, s1, [world(h, q, jj, ac) for jj in range(8) if not (h == 2 and jj == js)])
+        send(src, "asm", base, base + 128, [world(2, q, js, ac)])
+        for h in range(4):
+            for j in range(8):
+                final(world(h, q, j, ac), h, q, j, base, base + 128)
+    return sends, off
+
+
+def build_programs(widths, cores):
+    sends, off = build_sends(widths)
+    arrive, leave = {}, {}
+    for n, s in enumerate(sends):
+        leave.setdefault(s[0], []).append(n)
+        for d in s[4]:
+            arrive.setdefault(d, []).append(n)
+    need = []
+    for s in sends:
+        need.append(tuple(sorted(set(sends[a][1] for a in arrive.get(s[0], [])
+                                     if sends[a][2] < s[3] and s[2] < sends[a][3]))))
+    depth = {}
+
+    def depth_of(n):
+        if n not in depth:
+            depth[n] = -1
+            d = 0
+            for a in arrive.get(sends[n][0], []):
+                if sends[a][1] in need[n]:
+                    da = depth_of(a)
+                    if da < 0:
+                        raise ValueError("cycle")
+                    d = max(d, da)
+            depth[n] = d + 1
+        return depth[n]
+
+    calls = {}
+    engines = {}
+    for core, ns in leave.items():
+        groups = {}
+        for n in ns:
+            groups.setdefault((depth_of(n), need[n], sends[n][3] - sends[n][2]), []).append(n)
+        lst = []
+        for key in sorted(groups):
+            g = sorted(groups[key], key=lambda n: sends[n][2])
+            for k in range(0, len(g), 8):
+                part = g[k:k + 8]
+                e = 8
+                while e * len(part) > 8:
+                    e //= 2
+                for n in part:
+                    engines[n] = e
+                lst.append((key[1], part))
+        calls[core] = lst
+    progs = {}
+    for core in set(list(arrive) + list(leave) + list(cores)):
+        total = {}
+        for a in arrive.get(core, []):
+            total[sends[a][1]] = total.get(sends[a][1], 0) + engines[a]
+        prog, waited, sent = [], set(), 0
+        if core in cores:
+            r = cores.index(core)
+            prog.append(("load", off[r], off[r + 1]))
+        for nd, part in calls.get(core, []):
+            for sm in nd:
+                if sm not in waited:
+                    waited.add(sm)
+                    prog.append(("wait", sm, total[sm]))
+            trs, used = [], 0
+            for n in part:
+                e = engines[n]
+                trs.append((((1 << e) - 1) << used, sends[n][1], sends[n][2], sends[n][3], tuple(sends[n][4])))
+                used += e
+                sent += e
+            prog.append(("call", trs))
+        for sm in sorted(total):
+            if sm not in waited:
+                prog.append(("wait", sm, total[sm]))
+        if sent:
+            prog.append(("wait", "read", sent))
+        if core in cores:
+            prog.append(("store",))
+        progs[core] = prog
+    return progs
+
+
+def rank_program(g, core, T, topo):
+    if "p" not in CACHE:
+        CACHE["p"] = build_programs(list(T.tables["WIDTHS"]), list(T.cores))
+    prog = CACHE["p"].get(core)
+    if not prog:
+        return
+    sem = {"read": T.sem.read, "sh": T.sem.sh, "asm": T.sem.asm, "rl": T.sem.rl, "hf": T.sem.hf, "fin": T.sem.fin}
+    for step in prog:
+        if step[0] == "load":
+            g.dma_start(T.land[:, step[1]:step[2]], T.x[:, 0:step[2] - step[1]]).then_inc(T.sem.loaded, 16)
+            g.wait_ge(T.sem.loaded, 16)
+        elif step[0] == "wait":
+            g.wait_ge(sem[step[1]], step[2])
+        elif step[0] == "call":
+            trs = []
+            for mask, sm, c0, c1, dsts in step[1]:
+                ids = []
+                for d in dsts:
+                    rid, pid = topo.addr(d, core)
+                    ids.append(DstId(rid=rid, pnc=pid))
+                trs.append(RemoteDMATransfer(dst_ids=ids, dma_engine_mask=mask, remote_sem=sem[sm],
+                                             srcs=[T.land[:, c0:c1]], dsts=[T.land[:, c0:c1] for d in dsts]))
+            g.remote_dma_fused(trs, local_sem=T.sem.read)
+        else:
+            g.dma_start(T.y[:, :], T.land[:, :]).then_inc(T.sem.stored, 16)
+            g.wait_ge(T.sem.stored, 16)

@@ -4,7 +4,7 @@ TOTAL = 752
 SCRATCH = {
     "land": ("sbuf", [128, TOTAL], "float32"),
 }
-SEMAPHORES = ["loaded", "read", "stored", "sh", "asm", "rl", "hf", "fin"]
+SEMAPHORES = ["loaded", "read", "stored", "big", "small", "relay", "asm", "fin"]
 CACHE = {}
 
 
@@ -17,74 +17,98 @@ def build_sends(widths):
     for w in widths:
         off.append(off[-1] + w)
     sends = []
+    have = {}
+    for r in range(64):
+        have[world(r // 16, r % 2, (r % 16) // 2, 5)] = [(off[r], off[r + 1])]
 
     def send(src, sem, c0, c1, dsts):
         if dsts and c1 > c0:
             sends.append([src, sem, c0, c1, list(dsts)])
 
-    def final(asm_core, h, q, j, c0, c1):
-        full = []
+    def last_step(asm_core, h, q, j, c0, c1):
+        parts = {}
         for qq in (q, 1 - q):
-            r = 16 * h + 2 * j + qq
-            o0, o1 = off[r], off[r + 1]
             dst = world(h, qq, j, 5)
-            if o1 <= c0 or o0 >= c1:
-                full.append(dst)
-            else:
-                send(asm_core, "fin", c0, o0, [dst])
-                send(asm_core, "fin", o1, c1, [dst])
-        send(asm_core, "fin", c0, c1, full)
+            at = c0
+            for o0, o1 in sorted(have[dst]) + [(c1, c1)]:
+                if o1 <= c0 or o0 > c1:
+                    continue
+                if o0 > at:
+                    parts.setdefault((at, o0), []).append(dst)
+                at = max(at, o1)
+        for (a0, a1), dsts in sorted(parts.items()):
+            send(asm_core, "fin", a0, a1, dsts)
+
+    segments = []
 
     for x in range(4):
-        p = 0 if x < 2 else 1
-        c = 7 if x in (0, 2) else 3
-        js = [j for j in range(8) if widths[16 * x + 2 * j] == 4]
-        seg0, seg1 = off[16 * x + 2 * js[0]], off[16 * x + 16]
-        for j in js:
-            own = {h: world(h, p, j, c) for h in range(4)}
-            ox, oi, oc, od = own[x], own[x ^ 1], own[3 - x], own[x ^ 2]
+        p = x // 2
+        c = 7 if x % 2 == 0 else 3
+        pairs = [j for j in range(8) if widths[16 * x + 2 * j] == 4]
+        seg0, seg1 = off[16 * x + 2 * pairs[0]], off[16 * x + 16]
+        for j in pairs:
+            own = {}
+            for h in range(4):
+                scatters = widths[16 * h + 2 * j + p] > 4
+                own[h] = world(h, p, j, 1 if scatters and c == 7 else c)
+            home, near, cabled, fourth = own[x], own[x ^ 1], own[3 - x], own[x ^ 2]
             cs, co = off[16 * x + 2 * j + p], off[16 * x + 2 * j + 1 - p]
             p0 = min(cs, co)
-            first = [ox, oi] if x < 2 else [ox, oi, oc]
-            relay = world(x, 1 - p, j, 6)
-            send(world(x, p, j, 5), "hf", cs, cs + 4, first)
-            send(world(x, 1 - p, j, 5), "rl", co, co + 4, [relay])
-            send(relay, "hf", co, co + 4, first)
+            same, other = world(x, p, j, 5), world(x, 1 - p, j, 5)
+            r7, r3 = world(x, 1 - p, j, 7), world(x, 1 - p, j, 3)
+            send(r7, "small", co, co + 4, [home])
+            send(r3, "small", co, co + 4, [near])
             if x < 2:
-                send(ox, "hf", p0, p0 + 8, [oc])
-                send(oi, "hf", p0, p0 + 8, [od])
+                send(same, "small", cs, cs + 4, [home, near])
+                send(other, "relay", co, co + 4, [r7, r3])
+                send(home, "small", p0, p0 + 8, [cabled])
+                send(near, "small", p0, p0 + 8, [fourth])
             else:
-                send(oc, "hf", p0, p0 + 8, [od])
+                far = world(3 - x, 1 - p, j, 3 if x == 3 else 7)
+                far5 = world(3 - x, 1 - p, j, 5)
+                send(same, "small", cs, cs + 4, [home, near, cabled])
+                send(other, "relay", co, co + 4, [r7, r3, far])
+                send(far, "small", co, co + 4, [cabled])
+                send(far, "fin", co, co + 4, [far5])
+                have[far5].append((co, co + 4))
+                send(cabled, "small", p0, p0 + 8, [fourth])
             for h in range(4):
-                send(own[h], "asm", p0, p0 + 8, [world(h, p, jj, c) for jj in range(8) if jj != j])
+                send(own[h], "asm", p0, p0 + 8, [d for d in [world(h, p, jj, c) for jj in range(8)] if d != own[h]])
         for h in range(4):
             for j in range(8):
-                final(world(h, p, j, c), h, p, j, seg0, seg1)
+                segments.append((world(h, p, j, c), h, p, j, seg0, seg1))
 
     for i in range(4):
         q, js = i % 2, i // 2
         base = off[32 + i]
-        ac = 6 if i < 2 else 2
         src = world(2, q, js, 5)
+        asm = [2 if j % 2 == js % 2 else 6 for j in range(8)]
         for j in range(8):
             a = j % 2 == js % 2
             s0, s1 = base + 16 * j, base + 16 * j + 16
-            oc = {0: 0 if a else 4, 1: 0 if a else 4, 2: 0 if a else 4, 3: 4 if a else 0}
-            own = {h: world(h, q, j, oc[h]) for h in range(4)}
-            if a:
-                send(src, "sh", s0, s1, [own[2]])
-                send(own[2], "sh", s0, s1, [own[1], own[3]])
-                send(own[1], "sh", s0, s1, [own[0]])
+            own = {h: world(h, q, j, (4 if a else 0) if h == 3 else (0 if a else 4)) for h in range(4)}
+            if j == js:
+                own[2] = world(2, q, js, asm[js])
+                send(src, "big", s0, s1, [own[3]])
+                send(own[2], "big", s0, s1, [own[1]])
+                send(own[1], "big", s0, s1, [own[0]])
+            elif a:
+                send(src, "big", s0, s1, [own[2]])
+                send(own[2], "big", s0, s1, [own[1], own[3]])
+                send(own[1], "big", s0, s1, [own[0]])
             else:
-                send(src, "sh", s0, s1, [own[3]])
-                send(own[3], "sh", s0, s1, [own[2], own[0]])
-                send(own[0], "sh", s0, s1, [own[1]])
+                send(src, "big", s0, s1, [own[3]])
+                send(own[3], "big", s0, s1, [own[2], own[0]])
+                send(own[0], "big", s0, s1, [own[1]])
             for h in range(4):
-                send(own[h], "asm", s0, s1, [world(h, q, jj, ac) for jj in range(8) if not (h == 2 and jj == js)])
-        send(src, "asm", base, base + 128, [world(2, q, js, ac)])
+                send(own[h], "asm", s0, s1, [world(h, q, jj, asm[jj]) for jj in range(8) if not (h == 2 and jj == js)])
+        send(src, "asm", base, base + 128, [world(2, q, js, asm[js])])
         for h in range(4):
             for j in range(8):
-                final(world(h, q, j, ac), h, q, j, base, base + 128)
+                segments.append((world(h, q, j, asm[j]), h, q, j, base, base + 128))
+
+    for seg in segments:
+        last_step(*seg)
     return sends, off
 
 
@@ -109,22 +133,21 @@ def build_programs(widths, cores):
                 if sends[a][1] in need[n]:
                     da = depth_of(a)
                     if da < 0:
-                        raise ValueError("cycle")
+                        raise ValueError("the plan has a cycle")
                     d = max(d, da)
             depth[n] = d + 1
         return depth[n]
 
-    calls = {}
-    engines = {}
+    calls, engines = {}, {}
     for core, ns in leave.items():
         groups = {}
         for n in ns:
             groups.setdefault((depth_of(n), need[n], sends[n][3] - sends[n][2]), []).append(n)
         lst = []
         for key in sorted(groups):
-            g = sorted(groups[key], key=lambda n: sends[n][2])
-            for k in range(0, len(g), 8):
-                part = g[k:k + 8]
+            grp = sorted(groups[key], key=lambda n: sends[n][2])
+            for k in range(0, len(grp), 8):
+                part = grp[k:k + 8]
                 e = 8
                 while e * len(part) > 8:
                     e //= 2
@@ -132,6 +155,7 @@ def build_programs(widths, cores):
                     engines[n] = e
                 lst.append((key[1], part))
         calls[core] = lst
+
     progs = {}
     for core in set(list(arrive) + list(leave) + list(cores)):
         total = {}
@@ -170,7 +194,8 @@ def rank_program(g, core, T, topo):
     prog = CACHE["p"].get(core)
     if not prog:
         return
-    sem = {"read": T.sem.read, "sh": T.sem.sh, "asm": T.sem.asm, "rl": T.sem.rl, "hf": T.sem.hf, "fin": T.sem.fin}
+    sem = {"read": T.sem.read, "big": T.sem.big, "small": T.sem.small, "relay": T.sem.relay, "asm": T.sem.asm,
+           "fin": T.sem.fin}
     for step in prog:
         if step[0] == "load":
             g.dma_start(T.land[:, step[1]:step[2]], T.x[:, 0:step[2] - step[1]]).then_inc(T.sem.loaded, 16)

@@ -26,31 +26,32 @@ def build_sends(widths):
             sends.append([src, sem, c0, c1, list(dsts)])
 
     def last_step(asm_core, h, q, j, c0, c1):
-        parts = {}
-        for qq in (q, 1 - q):
-            dst = world(h, qq, j, 5)
-            at = c0
-            for o0, o1 in sorted(have[dst]) + [(c1, c1)]:
-                if o1 <= c0 or o0 > c1:
-                    continue
-                if o0 > at:
-                    parts.setdefault((at, o0), []).append(dst)
-                at = max(at, o1)
-        for (a0, a1), dsts in sorted(parts.items()):
-            send(asm_core, "fin", a0, a1, dsts)
+        dsts = [world(h, qq, j, 5) for qq in (q, 1 - q)]
+        holes = {d: [(max(o0, c0), min(o1, c1)) for o0, o1 in have[d] if o0 < c1 and c0 < o1] for d in dsts}
+        ways = []
+        for cut_all in (False, True):
+            parts = {}
+            for d in dsts:
+                cuts = sorted(set([c0, c1] + [e for dd in dsts if cut_all or dd == d for o in holes[dd] for e in o]))
+                for a0, a1 in zip(cuts, cuts[1:]):
+                    if not any(o0 <= a0 and a1 <= o1 for o0, o1 in holes[d]):
+                        parts.setdefault((a0, a1), []).append(d)
+            ways.append((len(set(a1 - a0 for a0, a1 in parts)), sum(len(v) for v in parts.values()), sorted(parts.items())))
+        for (a0, a1), to in min(ways)[2]:
+            send(asm_core, "fin", a0, a1, to)
 
     segments = []
 
     for x in range(4):
         p = x // 2
-        c = 7 if x % 2 == 0 else 3
+        asm = [3 if h in (x, 3 - x) else 7 for h in range(4)]
         pairs = [j for j in range(8) if widths[16 * x + 2 * j] == 4]
         seg0, seg1 = off[16 * x + 2 * pairs[0]], off[16 * x + 16]
         for j in pairs:
             own = {}
             for h in range(4):
                 scatters = widths[16 * h + 2 * j + p] > 4
-                own[h] = world(h, p, j, 1 if scatters and c == 7 else c)
+                own[h] = world(h, p, j, 1 if asm[h] == 3 else 0 if scatters else 7)
             home, near, cabled, fourth = own[x], own[x ^ 1], own[3 - x], own[x ^ 2]
             cs, co = off[16 * x + 2 * j + p], off[16 * x + 2 * j + 1 - p]
             p0 = min(cs, co)
@@ -64,8 +65,7 @@ def build_sends(widths):
                 send(home, "small", p0, p0 + 8, [cabled])
                 send(near, "small", p0, p0 + 8, [fourth])
             else:
-                far = world(3 - x, 1 - p, j, 3 if x == 3 else 7)
-                far5 = world(3 - x, 1 - p, j, 5)
+                far, far5 = world(3 - x, 1 - p, j, 3), world(3 - x, 1 - p, j, 5)
                 send(same, "small", cs, cs + 4, [home, near, cabled])
                 send(other, "relay", co, co + 4, [r7, r3, far])
                 send(far, "small", co, co + 4, [cabled])
@@ -73,10 +73,10 @@ def build_sends(widths):
                 have[far5].append((co, co + 4))
                 send(cabled, "small", p0, p0 + 8, [fourth])
             for h in range(4):
-                send(own[h], "asm", p0, p0 + 8, [d for d in [world(h, p, jj, c) for jj in range(8)] if d != own[h]])
+                send(own[h], "asm", p0, p0 + 8, [d for d in [world(h, p, jj, asm[h]) for jj in range(8)] if d != own[h]])
         for h in range(4):
             for j in range(8):
-                segments.append((world(h, p, j, c), h, p, j, seg0, seg1))
+                segments.append((world(h, p, j, asm[h]), h, p, j, seg0, seg1))
 
     for i in range(4):
         q, js = i % 2, i // 2

from concourse.bass import DstId, RemoteDMATransfer

TOTAL = 752
SCRATCH = {
    "land": ("sbuf", [128, TOTAL], "float32"),
}
SEMAPHORES = ["loaded", "read", "stored", "big", "small", "relay", "asm", "fin"]
CACHE = {}


def world(h, q, j, c):
    return h * 128 + (2 * j + q) * 8 + c


def build_sends(widths):
    off = [0]
    for w in widths:
        off.append(off[-1] + w)
    sends = []
    have = {}
    for r in range(64):
        have[world(r // 16, r % 2, (r % 16) // 2, 5)] = [(off[r], off[r + 1])]

    def send(src, sem, c0, c1, dsts):
        if dsts and c1 > c0:
            sends.append([src, sem, c0, c1, list(dsts)])

    def last_step(asm_core, h, q, j, c0, c1):
        dsts = [world(h, qq, j, 5) for qq in (q, 1 - q)]
        holes = {d: [(max(o0, c0), min(o1, c1)) for o0, o1 in have[d] if o0 < c1 and c0 < o1] for d in dsts}
        ways = []
        for cut_all in (False, True):
            parts = {}
            for d in dsts:
                cuts = sorted(set([c0, c1] + [e for dd in dsts if cut_all or dd == d for o in holes[dd] for e in o]))
                for a0, a1 in zip(cuts, cuts[1:]):
                    if not any(o0 <= a0 and a1 <= o1 for o0, o1 in holes[d]):
                        parts.setdefault((a0, a1), []).append(d)
            ways.append((len(set(a1 - a0 for a0, a1 in parts)), sum(len(v) for v in parts.values()), sorted(parts.items())))
        for (a0, a1), to in min(ways)[2]:
            send(asm_core, "fin", a0, a1, to)

    segments = []

    for x in range(4):
        p = x // 2
        asm = [3 if h in (x, 3 - x) else 7 for h in range(4)]
        pairs = [j for j in range(8) if widths[16 * x + 2 * j] == 4]
        seg0, seg1 = off[16 * x + 2 * pairs[0]], off[16 * x + 16]
        for j in pairs:
            own = {}
            for h in range(4):
                scatters = widths[16 * h + 2 * j + p] > 4
                own[h] = world(h, p, j, 1 if asm[h] == 3 else 0 if scatters else 7)
            home, near, cabled, fourth = own[x], own[x ^ 1], own[3 - x], own[x ^ 2]
            cs, co = off[16 * x + 2 * j + p], off[16 * x + 2 * j + 1 - p]
            p0 = min(cs, co)
            same, other = world(x, p, j, 5), world(x, 1 - p, j, 5)
            r7, r3 = world(x, 1 - p, j, 7), world(x, 1 - p, j, 3)
            send(r7, "small", co, co + 4, [home])
            send(r3, "small", co, co + 4, [near])
            if x < 2:
                send(same, "small", cs, cs + 4, [home, near])
                send(other, "relay", co, co + 4, [r7, r3])
                send(home, "small", p0, p0 + 8, [cabled])
                send(near, "small", p0, p0 + 8, [fourth])
            else:
                far, far5 = world(3 - x, 1 - p, j, 3), world(3 - x, 1 - p, j, 5)
                send(same, "small", cs, cs + 4, [home, near, cabled])
                send(other, "relay", co, co + 4, [r7, r3, far])
                send(far, "small", co, co + 4, [cabled])
                send(far, "fin", co, co + 4, [far5])
                have[far5].append((co, co + 4))
                send(cabled, "small", p0, p0 + 8, [fourth])
            for h in range(4):
                send(own[h], "asm", p0, p0 + 8, [d for d in [world(h, p, jj, asm[h]) for jj in range(8)] if d != own[h]])
        for h in range(4):
            for j in range(8):
                segments.append((world(h, p, j, asm[h]), h, p, j, seg0, seg1))

    for i in range(4):
        q, js = i % 2, i // 2
        base = off[32 + i]
        src = world(2, q, js, 5)
        asm = [2 if j % 2 == js % 2 else 6 for j in range(8)]
        for j in range(8):
            a = j % 2 == js % 2
            s0, s1 = base + 16 * j, base + 16 * j + 16
            own = {h: world(h, q, j, (4 if a else 0) if h == 3 else (0 if a else 4)) for h in range(4)}
            if j == js:
                own[2] = world(2, q, js, asm[js])
                send(src, "big", s0, s1, [own[3]])
                send(own[2], "big", s0, s1, [own[1]])
                send(own[1], "big", s0, s1, [own[0]])
            elif a:
                send(src, "big", s0, s1, [own[2]])
                send(own[2], "big", s0, s1, [own[1], own[3]])
                send(own[1], "big", s0, s1, [own[0]])
            else:
                send(src, "big", s0, s1, [own[3]])
                send(own[3], "big", s0, s1, [own[2], own[0]])
                send(own[0], "big", s0, s1, [own[1]])
            for h in range(4):
                send(own[h], "asm", s0, s1, [world(h, q, jj, asm[jj]) for jj in range(8) if not (h == 2 and jj == js)])
        send(src, "asm", base, base + 128, [world(2, q, js, asm[js])])
        for h in range(4):
            for j in range(8):
                segments.append((world(h, q, j, asm[j]), h, q, j, base, base + 128))

    for seg in segments:
        last_step(*seg)
    return sends, off


def build_programs(widths, cores):
    sends, off = build_sends(widths)
    arrive, leave = {}, {}
    for n, s in enumerate(sends):
        leave.setdefault(s[0], []).append(n)
        for d in s[4]:
            arrive.setdefault(d, []).append(n)
    need = []
    for s in sends:
        need.append(tuple(sorted(set(sends[a][1] for a in arrive.get(s[0], [])
                                     if sends[a][2] < s[3] and s[2] < sends[a][3]))))
    depth = {}

    def depth_of(n):
        if n not in depth:
            depth[n] = -1
            d = 0
            for a in arrive.get(sends[n][0], []):
                if sends[a][1] in need[n]:
                    da = depth_of(a)
                    if da < 0:
                        raise ValueError("the plan has a cycle")
                    d = max(d, da)
            depth[n] = d + 1
        return depth[n]

    calls, engines = {}, {}
    for core, ns in leave.items():
        groups = {}
        for n in ns:
            groups.setdefault((depth_of(n), need[n], sends[n][3] - sends[n][2]), []).append(n)
        lst = []
        for key in sorted(groups):
            grp = sorted(groups[key], key=lambda n: sends[n][2])
            for k in range(0, len(grp), 8):
                part = grp[k:k + 8]
                e = 8
                while e * len(part) > 8:
                    e //= 2
                for n in part:
                    engines[n] = e
                lst.append((key[1], part))
        calls[core] = lst

    progs = {}
    for core in set(list(arrive) + list(leave) + list(cores)):
        total = {}
        for a in arrive.get(core, []):
            total[sends[a][1]] = total.get(sends[a][1], 0) + engines[a]
        prog, waited, sent = [], set(), 0
        if core in cores:
            r = cores.index(core)
            prog.append(("load", off[r], off[r + 1]))
        for nd, part in calls.get(core, []):
            for sm in nd:
                if sm not in waited:
                    waited.add(sm)
                    prog.append(("wait", sm, total[sm]))
            trs, used = [], 0
            for n in part:
                e = engines[n]
                trs.append((((1 << e) - 1) << used, sends[n][1], sends[n][2], sends[n][3], tuple(sends[n][4])))
                used += e
                sent += e
            prog.append(("call", trs))
        for sm in sorted(total):
            if sm not in waited:
                prog.append(("wait", sm, total[sm]))
        if sent:
            prog.append(("wait", "read", sent))
        if core in cores:
            prog.append(("store",))
        progs[core] = prog
    return progs


def rank_program(g, core, T, topo):
    if "p" not in CACHE:
        CACHE["p"] = build_programs(list(T.tables["WIDTHS"]), list(T.cores))
    prog = CACHE["p"].get(core)
    if not prog:
        return
    sem = {"read": T.sem.read, "big": T.sem.big, "small": T.sem.small, "relay": T.sem.relay, "asm": T.sem.asm,
           "fin": T.sem.fin}
    for step in prog:
        if step[0] == "load":
            g.dma_start(T.land[:, step[1]:step[2]], T.x[:, 0:step[2] - step[1]]).then_inc(T.sem.loaded, 16)
            g.wait_ge(T.sem.loaded, 16)
        elif step[0] == "wait":
            g.wait_ge(sem[step[1]], step[2])
        elif step[0] == "call":
            trs = []
            for mask, sm, c0, c1, dsts in step[1]:
                ids = []
                for d in dsts:
                    rid, pid = topo.addr(d, core)
                    ids.append(DstId(rid=rid, pnc=pid))
                trs.append(RemoteDMATransfer(dst_ids=ids, dma_engine_mask=mask, remote_sem=sem[sm],
                                             srcs=[T.land[:, c0:c1]], dsts=[T.land[:, c0:c1] for d in dsts]))
            g.remote_dma_fused(trs, local_sem=T.sem.read)
        else:
            g.dma_start(T.y[:, :], T.land[:, :]).then_inc(T.sem.stored, 16)
            g.wait_ge(T.sem.stored, 16)
